import numpy as np
import ml_dtypes


def mxq(x, axis, fmt="e4m3"):
    dtype, down = {"e4m3": (ml_dtypes.float8_e4m3fn, 7), "e5m2": (ml_dtypes.float8_e5m2, 14)}[fmt]
    v = np.moveaxis(np.asarray(x, np.float32).astype(ml_dtypes.bfloat16).astype(np.float64), axis, -1)
    blocks = v.reshape(v.shape[:-1] + (-1, 32))
    amax = np.abs(blocks).max(-1, keepdims=True)
    byte = np.maximum(np.where(amax > 0, np.frexp(amax)[1] - 1 + 127, 0) - down, 1)
    scale = np.exp2(byte - 127.0)
    codes = (blocks / scale).astype(np.float32).astype(dtype).astype(np.float64)
    return np.moveaxis((codes * scale).reshape(v.shape), -1, axis)


WIDE = False


def mx_kscale(k):
    if not WIDE:
        return np.ones(k)
    levels = np.array([10, -10, 5, -5, 0])
    if k % 512:
        return np.exp2(np.random.permutation(np.resize(levels, k // 32))).repeat(32)
    a = np.empty((k // 512, 16))
    for p in range(k // 512):
        a[p, :8] = np.random.permutation(np.resize(levels, 8))
        for g in range(8):
            far = levels[np.abs(levels - a[p, g]) >= 10]
            a[p, g + 8] = far[np.random.randint(len(far))]
    return np.exp2(a.ravel()).repeat(32)


BF16 = ml_dtypes.bfloat16


def bf(x):
    return np.asarray(x, np.float32).astype(BF16)


def f64(x):
    return np.asarray(x).astype(np.float64)


E2M1 = np.array([0.0, 0.5, 1.0, 1.5, 2.0, 3.0, 4.0, 6.0, -0.0, -0.5, -1.0, -1.5, -2.0, -3.0, -4.0, -6.0])


def pack_weight(w, fmt):
    k, n = w.shape
    w = f64(bf(w)).reshape(k // 32, 32, n)
    amax = np.abs(w).max(1)
    if fmt == "e4m3":
        byte = np.frexp(amax)[1] - 1 + 127 - 7
    else:
        mant, ex = np.frexp(amax / 6.0)
        byte = np.where(mant > 0.5, ex, ex - 1) + 127
    byte = np.clip(np.where(amax > 0, byte, 1), 1, 254)
    scaled = (w * np.exp2(127.0 - byte)[:, None, :]).reshape(k, n).astype(np.float32)
    by_word = np.ascontiguousarray(scaled.reshape(k // 512, 128, 4, n).transpose(0, 1, 3, 2))
    if fmt == "e4m3":
        words = by_word.astype(ml_dtypes.float8_e4m3fn).view(np.uint8)
    else:
        c = by_word.astype(ml_dtypes.float4_e2m1fn).view(np.uint8) & 0xF
        words = c[..., 0::2] | (c[..., 1::2] << 4)
    return np.ascontiguousarray(words), np.ascontiguousarray(byte.astype(np.uint8).reshape(k // 512, 16, n))


def unpack_weight(words, scales, fmt):
    g, p, n, _ = words.shape
    if fmt == "e4m3":
        vals = np.ascontiguousarray(words).view(ml_dtypes.float8_e4m3fn).astype(np.float64)
    else:
        nib = np.empty((g, p, n, 4), np.uint8)
        nib[..., 0::2] = words & 0xF
        nib[..., 1::2] = words >> 4
        vals = E2M1[nib]
    vals = vals * np.repeat(np.exp2(scales.astype(np.float64) - 127.0), 8, axis=1)[..., None]
    return vals.transpose(0, 1, 3, 2).reshape(g * 512, n)
def pack4(w):
    words, scales = pack_weight(w, "e2m1")
    return words.reshape(words.shape[0], 128, -1), scales


def unpack4(words, scales):
    return unpack_weight(words.reshape(words.shape[0], 128, -1, 2), scales, "e2m1")


def planes(Y):
    n, m = Y.shape
    b = f64(bf(Y)).reshape(n // 32, 32, m)
    amax = np.abs(b).max(1)
    byte = np.clip(np.where(amax > 0, np.frexp(amax)[1] - 1 + 127 - 7, 1), 1, 254)
    codes = (b * np.exp2(127.0 - byte)[:, None, :]).reshape(n, m).astype(np.float32).astype(ml_dtypes.float8_e4m3fn).view(np.uint8)
    words = codes.reshape(n // 512, 128, 4, m).transpose(0, 1, 3, 2)
    return np.ascontiguousarray(words), np.ascontiguousarray(byte.astype(np.uint8).reshape(n // 512, 16, m))


J, N, Q = 1024, 1024, 1536
ALPHA, CROSS, CHB, HB2 = 0.3, 0.5, 0.8, 0.1

def misfit(s, o, s2, o2):
    x = s[:, None] + s2[None, :]
    return ALPHA * x * (x + CROSS * (o[:, None] + o2[None, :]))

def bond(s, s2):
    return CHB * np.minimum(0.0, s[:, None] * s2[None, :] + HB2)

def setup_inputs():
    t1, t2 = mx_kscale(N), mx_kscale(N)
    s, o = np.random.uniform(-1.5, 1.5, N), np.random.uniform(-1.0, 1.0, N)
    sp, op = np.random.uniform(-1.5, 1.5, Q), np.random.uniform(-1.0, 1.0, Q)
    c = np.random.uniform(-1.5, 1.5, J)
    a = np.exp(0.3 * np.random.randn(N)) / N
    d = np.exp(-0.5 * (s[None, :] - c[:, None]) ** 2 + 0.5 * np.random.randn(J, N))
    d = d / (d * a[None, :]).sum(axis=1, keepdims=True)
    g0 = np.exp(0.5 * np.random.randn(J, N))
    e = misfit(s, o, s, o)
    h = (a / t1)[:, None] * np.exp(-e) * (np.exp(-bond(s, s)) - 1.0)
    f = (a / t2)[:, None] * np.exp(-misfit(s, o, sp, op) - bond(s, sp))
    h_words, h_scales = pack4(h)
    f_words, f_scales = pack_weight(f, "e4m3")
    return {"profile": bf(d * t2[None, :]), "start": bf(g0 * (t1 / t2)[None, :]),
            "energy": bf(e), "width": bf(a / t1), "h_words": h_words, "h_scales": h_scales,
            "f_words": f_words, "f_scales": f_scales, "probe": bf(np.exp(0.7 * np.random.randn(Q)))}

def reference(profile, start, energy, width, h_words, h_scales, f_words, f_scales, probe):
    p = f64(profile)
    w = mxq(p * f64(start), 1, "e4m3")
    tau = f64(width)[:, None] * np.exp(-f64(energy))
    S = (w @ mxq(tau, 0, "e4m3")) + (w @ unpack4(h_words, h_scales))
    v = p / S
    R = mxq(v, 1, "e4m3") @ unpack_weight(f_words, f_scales, "e4m3")
    y = f64(probe)[None, :] / R
    Y = y.T
    words, scales = planes(Y)
    return y, words, scales

@@ -1,0 +1,401 @@
+from contextlib import ExitStack
+
+import concourse.mybir as mybir
+from concourse.masks import make_identity
+
+J, N, Q = 1024, 1024, 1536
+FLOPS = 2 * J * N * (2 * N + Q)
+
+F32 = mybir.dt.float32
+BF16 = mybir.dt.bfloat16
+I32 = mybir.dt.int32
+U8 = mybir.dt.uint8
+FP8X4 = mybir.dt.float8_e4m3fn_x4
+FP4X4 = mybir.dt.float4_e2m1fn_x4
+ACT = mybir.ActivationFunctionType
+MULT = mybir.AluOpType.mult
+
+P = 128
+PACK = 4
+KP = P * PACK
+KG = N // KP
+RG = Q // KP
+JT = J // P
+GJ = 2
+NG = JT // GJ
+NJ = GJ * P
+
+
+def tile_cosmo_segment_activities_k6_kernel(
+    tc, profile, start, energy, width, h_words, h_scales, f_words, f_scales, probe, out_0, out_1, out_2
+):
+    nc = tc.nc
+    with ExitStack() as ctx:
+        keep = ctx.enter_context(tc.tile_pool(name="keep", bufs=1))
+        work = ctx.enter_context(tc.tile_pool(name="work", bufs=3))
+        psum = ctx.enter_context(tc.psum_pool(name="psum", bufs=8))
+        ctx.enter_context(tc.manual_schedule())
+
+        def kept(shape, dtype, name):
+            return keep.tile(shape, dtype, name=name, align_bytes=64)
+
+        def passing(shape, dtype, name, bufs=3):
+            return work.tile(shape, dtype, name=name, bufs=bufs, align_bytes=64)
+
+        def bank(shape):
+            return psum.tile(shape, F32, name="bank")
+
+        ident = kept([P, P], F32, "ident")
+        one = kept([P, 1], F32, "one")
+        warm = kept([P, 1], F32, "warm")
+        width_sb = kept([P, KG, PACK], BF16, "width_sb")
+        ln_width = kept([P, KG, PACK], F32, "ln_width")
+        probe_sb = kept([P, RG, PACK], BF16, "probe_sb")
+        probe_rsqrt = kept([P, RG, PACK], F32, "probe_rsqrt")
+        probe_inv = kept([P, RG, PACK], F32, "probe_inv")
+        h_scale = kept([P, KG, N], U8, "h_scale")
+        f_scale_raw = kept([P, Q], U8, "f_scale_raw")
+        f_scale = kept([P, Q], U8, "f_scale")
+        y_scale = [kept([P, RG, J // 2], U8, "y_scale%d" % n) for n in range(2)]
+        e_raw = {(h, g): kept([P, PACK, KP], BF16, "e_raw%d%d" % (h, g)) for h in range(KG) for g in range(KG)}
+        tau_code = {(h, g): kept([P, KP], I32, "tau_code%d%d" % (h, g)) for h in range(KG) for g in range(KG)}
+        tau_scale = {(h, g): kept([P, KP], U8, "tau_scale%d%d" % (h, g)) for h in range(KG) for g in range(KG)}
+        h_code = [kept([P, 2 * N], U8, "h_code%d" % g) for g in range(KG)]
+        f_raw = [kept([P, Q], I32, "f_raw%d" % g) for g in range(KG)]
+        f_code = [kept([P, Q], I32, "f_code%d" % g) for g in range(KG)]
+        p_sb = [kept([P, N], BF16, "p_sb%d" % j) for j in range(JT)]
+        s_sb = [kept([P, N], BF16, "s_sb%d" % j) for j in range(JT)]
+        w_code = [kept([P, KG, P], I32, "w_code%d" % j) for j in range(JT)]
+        w_scale = [kept([P, KG, P], U8, "w_scale%d" % j) for j in range(JT)]
+        v_code = {(n, g): kept([P, NJ], I32, "v_code%d%d" % (n, g)) for n in range(NG) for g in range(KG)}
+        v_scale = {(n, g): kept([P, NJ], U8, "v_scale%d%d" % (n, g)) for n in range(NG) for g in range(KG)}
+        live = {}
+
+        def by_pair(ap):
+            return ap.rearrange("j (gm u e) -> j u gm e", u=2, e=2)
+
+        def as_pairs(ap):
+            return ap.rearrange("j (u gm e) -> j u gm e", u=2, e=2)
+
+        def load_e(h, g):
+            rows = energy[g * KP : (g + 1) * KP, h * KP : (h + 1) * KP]
+            nc.sync.dma_start(out=e_raw[h, g][:], in_=rows.rearrange("(p t) l -> p t l", t=PACK))
+
+        def load_ps(j):
+            nc.sync.dma_start(out=p_sb[j][:], in_=profile[j * P : (j + 1) * P, :])
+            nc.sync.dma_start(out=s_sb[j][:], in_=start[j * P : (j + 1) * P, :])
+
+        def tau_exp(h, g):
+            rows = passing([P, PACK, KP], BF16, "tau_rows")
+            for t in range(PACK):
+                nc.scalar.activation(
+                    out=rows[:, t, :], in_=e_raw[h, g][:, t, :], func=ACT.Exp, scale=-1.0, bias=ln_width[:, g, t : t + 1]
+                )
+            live["tau_rows", h, g] = rows
+
+        def tau_group(h, g):
+            grouped = passing([P, PACK * KP], BF16, "tau_grouped", bufs=2)
+            nc.vector.tensor_copy(
+                out=grouped[:].rearrange("p (c i t) -> p c t i", i=4, t=PACK),
+                in_=live["tau_rows", h, g][:].rearrange("p t (c i) -> p c t i", i=4),
+            )
+            live["tau_grouped", h, g] = grouped
+
+        def tau_quant(h, g):
+            nc.vector.quantize_mx(
+                out=tau_code[h, g][:].bitcast(FP8X4), scales=tau_scale[h, g][:], in_=live["tau_grouped", h, g][:]
+            )
+
+        def w_mul(j):
+            rows = passing([P, N], BF16, "rows")
+            nc.vector.tensor_tensor(out=as_pairs(rows[:]), in0=by_pair(p_sb[j][:]), in1=by_pair(s_sb[j][:]), op=MULT)
+            live["rows", "w", j] = rows
+
+        def turn(kind, j):
+            words = live["rows", kind, j][:].bitcast(F32)
+            turned = bank([P, KG, 2, P])
+            for g in range(KG):
+                for u in range(2):
+                    first = (u * KG + g) * P
+                    nc.tensor.transpose(turned[:, g, u, :], words[:, first : first + P], ident[:])
+            live["turned", kind, j] = turned
+
+        def gather(kind, j, on_scalar):
+            grouped = passing([P, N], BF16, "grouped")
+            dst = grouped[:].bitcast(F32).rearrange("p (g j u) -> p g j u", g=KG, u=2)
+            src = live["turned", kind, j][:].rearrange("p g u j -> p g j u")
+            if on_scalar:
+                nc.scalar.copy(out=dst, in_=src)
+            else:
+                nc.vector.tensor_copy(out=dst, in_=src)
+            live["grouped", kind, j] = grouped
+
+        def w_quant(j):
+            nc.vector.quantize_mx(
+                out=w_code[j][:].rearrange("p g j -> p (g j)").bitcast(FP8X4),
+                scales=w_scale[j][:].rearrange("p g j -> p (g j)"),
+                in_=live["grouped", "w", j][:],
+            )
+
+        def s_excess(j, h):
+            acc = bank([P, KP])
+            for g in range(KG):
+                nc.tensor.matmul_mx(
+                    out=acc[:], lhsT=w_code[j][:, g, :].bitcast(FP8X4), lhsT_scale=w_scale[j][:, g, :],
+                    rhs=h_code[g][:, 2 * h * KP : 2 * (h + 1) * KP].bitcast(FP4X4),
+                    rhs_scale=h_scale[:, g, h * KP : (h + 1) * KP], start=(g == 0), stop=False,
+                )
+            live["s_acc", j, h] = acc
+
+        def s_misfit(j, h, g):
+            nc.tensor.matmul_mx(
+                out=live["s_acc", j, h][:], lhsT=w_code[j][:, g, :].bitcast(FP8X4), lhsT_scale=w_scale[j][:, g, :],
+                rhs=tau_code[h, g][:].bitcast(FP8X4), rhs_scale=tau_scale[h, g][:], start=False, stop=(g == KG - 1),
+            )
+
+        def s_matmul(j, h):
+            s_excess(j, h)
+            for g in range(KG):
+                s_misfit(j, h, g)
+
+        def s_rsqrt(j, h):
+            if h == 0:
+                live["s_root", j] = passing([P, N], F32, "s_root", bufs=4)
+            dst = live["s_root", j][:, h * KP : (h + 1) * KP]
+            nc.scalar.activation(out=dst, in_=live["s_acc", j, h][:], func=ACT.Abs_reciprocal_sqrt)
+
+        def v_first(j, on_scalar):
+            half = passing([P, N], F32, "v_half")
+            root = live["s_root", j]
+            if on_scalar:
+                nc.scalar.activation(out=half[:], in_=root[:], func=ACT.Square)
+                live["v_other", j] = p_sb[j]
+            else:
+                nc.vector.tensor_tensor(out=half[:], in0=root[:], in1=p_sb[j][:], op=MULT)
+                live["v_other", j] = root
+            live["v_half", j] = half
+
+        def v_mul(j):
+            rows = passing([P, N], BF16, "rows")
+            nc.vector.tensor_tensor(out=as_pairs(rows[:]), in0=by_pair(live["v_half", j][:]), in1=by_pair(live["v_other", j][:]), op=MULT)
+            live["rows", "v", j] = rows
+
+        def v_quant(j):
+            n, first = j // GJ, (j % GJ) * P
+            for g in range(KG):
+                nc.vector.quantize_mx(
+                    out=v_code[n, g][:, first : first + P].bitcast(FP8X4), scales=v_scale[n, g][:, first : first + P],
+                    in_=live["grouped", "v", j][:, g * KP : (g + 1) * KP],
+                )
+
+        def f_sort(g):
+            nc.vector.tensor_copy(
+                out=f_code[g][:].rearrange("p (G t c i) -> p G c t i", G=RG, t=PACK, i=4),
+                in_=f_raw[g][:].rearrange("p (G c i t) -> p G c t i", G=RG, t=PACK, i=4),
+            )
+
+        def f_sort_scales():
+            nc.vector.tensor_copy(
+                out=f_scale[:].rearrange("p (G t m) -> p G t m", G=RG, t=PACK),
+                in_=f_scale_raw[:].rearrange("p (G m t) -> p G t m", G=RG, t=PACK),
+            )
+
+        def r_matmul(n, G, u):
+            acc = bank([P, 2, NJ])
+            for e in range(2):
+                first = G * KP + (2 * u + e) * P
+                for g in range(KG):
+                    nc.tensor.matmul_mx(
+                        out=acc[:, e, :], lhsT=f_code[g][:, first : first + P].bitcast(FP8X4),
+                        lhsT_scale=f_scale[PACK * g :, first : first + P],
+                        rhs=v_code[n, g][:].bitcast(FP8X4), rhs_scale=v_scale[n, g][:], start=(g == 0), stop=(g == KG - 1),
+                    )
+            live["r_acc", n, G, u] = acc
+
+        def y_rsqrt(n, G, u):
+            if u == 0:
+                live["y_root", n, G] = passing([P, PACK, NJ], F32, "y_root", bufs=6)
+            for e in range(2):
+                t = 2 * u + e
+                nc.scalar.activation(
+                    out=live["y_root", n, G][:, t, :], in_=live["r_acc", n, G, u][:, e, :], func=ACT.Abs_reciprocal_sqrt,
+                    scale=probe_inv[:, G, t : t + 1],
+                )
+
+        def y_turn(n, G, i):
+            turned = bank([P, PACK, P])
+            for t in range(PACK):
+                nc.tensor.transpose(turned[:, t, :], live["y_root", n, G][:, t, i * P : (i + 1) * P], ident[:])
+            live["y_turned", n, G, i] = turned
+
+        def y_store(n, G, i):
+            if i == 0:
+                live["y", n, G] = passing([P, GJ, KP], F32, "y", bufs=4)
+            y = live["y", n, G]
+            nc.scalar.activation(
+                out=y[:, i, :].rearrange("j (m t) -> j m t", t=PACK),
+                in_=live["y_turned", n, G, i][:].rearrange("j t m -> j m t"), func=ACT.Square,
+            )
+            if (n, G) == (NG - 1, RG - 1):
+                j = n * GJ + i
+                nc.sync.dma_start(out=out_0[j * P : (j + 1) * P, G * KP : (G + 1) * KP], in_=y[:, i, :])
+            elif i == GJ - 1:
+                rows = out_0[n * NJ : (n + 1) * NJ, G * KP : (G + 1) * KP]
+                nc.sync.dma_start(out=rows.rearrange("(i j) r -> j i r", j=P), in_=y[:])
+
+        def y_group(n, G):
+            grouped = passing([P, PACK * NJ], BF16, "y_grouped", bufs=3)
+            root = live["y_root", n, G][:].rearrange("p t (c i) -> p c t i", i=2)
+            nc.vector.tensor_tensor(
+                out=grouped[:].rearrange("p (c i t) -> p c t i", i=2, t=PACK), in0=root, in1=root, op=MULT
+            )
+            live["y_grouped", n, G] = grouped
+
+        def y_quant(n, G):
+            code = passing([P, NJ], I32, "y_code", bufs=4)
+            nc.vector.quantize_mx(out=code[:].bitcast(FP8X4), scales=y_scale[n // 2][:, G, (n % 2) * NJ : (n % 2 + 1) * NJ], in_=live["y_grouped", n, G][:])
+            words = out_1[G].rearrange("p m t -> p (m t)").bitcast(I32)
+            nc.sync.dma_start(out=words[:, n * NJ : (n + 1) * NJ], in_=code[:])
+
+        def y_store_scales(n):
+            for q in range(4):
+                rows = out_2[:, 4 * q : 4 * q + 4, n * J // 2 : (n + 1) * J // 2].rearrange("G r m -> r G m")
+                nc.sync.dma_start(out=rows.bitcast(I32), in_=y_scale[n][32 * q : 32 * q + 4, :, :].bitcast(I32))
+
+        nc.vector.memset(one[:], 1.0)
+        nc.vector.memset(h_scale[:].bitcast(I32), 0)
+        nc.vector.memset(f_scale_raw[:].bitcast(I32), 0)
+        nc.scalar.activation(out=warm[:], in_=one[:], func=ACT.Ln)
+        for q in range(4):
+            rows = h_scales[:, 4 * q : 4 * q + 4, :].rearrange("g r n -> r g n")
+            nc.gpsimd.dma_start(out=h_scale[32 * q : 32 * q + 4, :, :].bitcast(I32), in_=rows.bitcast(I32))
+        make_identity(nc, ident[:])
+        nc.sync.dma_start(out=width_sb[:], in_=width.rearrange("(g p t) -> p g t", p=P, t=PACK))
+        load_e(0, 0)
+        load_ps(0)
+        load_e(0, 1)
+        load_ps(1)
+        load_e(1, 0)
+        for g in range(KG):
+            nc.sync.dma_start(out=h_code[g][:].bitcast(I32), in_=h_words[g].bitcast(I32))
+        load_e(1, 1)
+        nc.sync.dma_start(out=probe_sb[:], in_=probe.rearrange("(G p t) -> p G t", p=P, t=PACK))
+        load_ps(2)
+        load_ps(3)
+        for q in range(4):
+            nc.sync.dma_start(
+                out=f_scale_raw[32 * q : 32 * q + 8, :].bitcast(I32), in_=f_scales[:, 4 * q : 4 * q + 4, :].bitcast(I32)
+            )
+        for g in range(KG):
+            nc.sync.dma_start(out=f_raw[g][:], in_=f_words[g].rearrange("p n t -> p (n t)").bitcast(I32))
+        for j in range(4, JT):
+            load_ps(j)
+
+        nc.scalar.activation(out=ln_width[:], in_=width_sb[:], func=ACT.Ln)
+        nc.scalar.activation(out=warm[:], in_=one[:], func=ACT.Exp)
+
+        tau_exp(0, 0)
+        w_mul(0)
+        turn("w", 0)
+        gather("w", 0, False)
+        tau_group(0, 0)
+        w_quant(0)
+        w_mul(1)
+        turn("w", 1)
+        tau_quant(0, 0)
+        tau_exp(0, 1)
+        tau_group(0, 1)
+        gather("w", 1, False)
+        tau_quant(0, 1)
+        s_matmul(0, 0)
+        w_quant(1)
+        s_matmul(1, 0)
+        s_excess(0, 1)
+        s_excess(1, 1)
+        tau_exp(1, 0)
+        tau_group(1, 0)
+        w_mul(2)
+        turn("w", 2)
+        tau_quant(1, 0)
+        s_misfit(0, 1, 0)
+        s_misfit(1, 1, 0)
+        tau_exp(1, 1)
+        nc.scalar.activation(out=probe_rsqrt[:], in_=probe_sb[:], func=ACT.Abs_reciprocal_sqrt)
+        tau_group(1, 1)
+        gather("w", 2, True)
+        s_rsqrt(0, 0)
+        s_rsqrt(1, 0)
+        w_quant(2)
+        tau_quant(1, 1)
+        s_excess(2, 0)
+        s_misfit(0, 1, 1)
+        s_misfit(1, 1, 1)
+        w_mul(3)
+        nc.vector.tensor_tensor(out=probe_inv[:], in0=probe_rsqrt[:], in1=probe_rsqrt[:], op=MULT)
+        s_rsqrt(0, 1)
+        s_rsqrt(1, 1)
+        v_first(0, True)
+        s_misfit(2, 0, 0)
+        s_misfit(2, 0, 1)
+        turn("w", 3)
+        f_sort(0)
+
+        halves = [(n, G, u) for n in range(NG) for G in range(RG) for u in range(2)]
+        R0 = 4
+        CU = 5
+
+        def thirds(first):
+            return halves[max(first, 0) : max(first + 3, 0)]
+
+        def mul_tiles(k):
+            return [j for j in range(JT) if k == (j + 2 if j < CU else j + 1)]
+
+        for k in range(2, JT + R0 + 3):
+            for j in mul_tiles(k - 1):
+                gather("v", j, k < 8)
+            if k + 1 < JT:
+                gather("w", k + 1, k < 4)
+            if CU <= k - 1 < JT and not (False):
+                v_first(k - 1, False)
+            if k - 2 < CU:
+                v_mul(k - 2)
+            for j in mul_tiles(k - 1):
+                v_quant(j)
+            if k + 1 < JT:
+                w_quant(k + 1)
+            if CU <= k - 1 < JT:
+                v_mul(k - 1)
+            if k + 2 < JT:
+                w_mul(k + 2)
+            if k == 2:
+                f_sort(1)
+            if k == 3:
+                f_sort_scales()
+            if k - 1 < CU:
+                v_first(k - 1, True)
+            done = [(n, G) for (n, G, u) in thirds(3 * (k - R0 - 1)) if u == 1]
+            for item in thirds(3 * (k - R0 - 2) - 1):
+                y_store(*item)
+            if k < JT:
+                if k > 2:
+                    s_matmul(k, 0)
+                s_matmul(k, 1)
+                s_rsqrt(k, 0)
+                s_rsqrt(k, 1)
+                if k >= CU and (False):
+                    v_first(k, True)
+            for item in thirds(3 * (k - R0)):
+                r_matmul(*item)
+                y_rsqrt(*item)
+            for un in done:
+                y_group(*un)
+            if k + 2 < JT:
+                turn("w", k + 2)
+            for j in mul_tiles(k):
+                turn("v", j)
+            for item in thirds(3 * (k - R0 - 1) - 1):
+                y_turn(*item)
+            for un in done:
+                y_quant(*un)
+                if un[1] == RG - 1 and un[0] % 2 == 1:
+                    y_store_scales(un[0] // 2)

@@ -34,20 +34,17 @@ def tile_cosmo_segment_activities_k6_kernel(
         keep = ctx.enter_context(tc.tile_pool(name="keep", bufs=1))
         work = ctx.enter_context(tc.tile_pool(name="work", bufs=3))
         psum = ctx.enter_context(tc.psum_pool(name="psum", bufs=8))
-        ctx.enter_context(tc.manual_schedule())
 
         def kept(shape, dtype, name):
             return keep.tile(shape, dtype, name=name, align_bytes=64)
 
-        def passing(shape, dtype, name, bufs=3):
-            return work.tile(shape, dtype, name=name, bufs=bufs, align_bytes=64)
+        def passing(shape, dtype, name, bufs=3, tag=None):
+            return work.tile(shape, dtype, name=name, tag=tag or name, bufs=bufs, align_bytes=64)
 
         def bank(shape):
             return psum.tile(shape, F32, name="bank")
 
         ident = kept([P, P], F32, "ident")
-        one = kept([P, 1], F32, "one")
-        warm = kept([P, 1], F32, "warm")
         width_sb = kept([P, KG, PACK], BF16, "width_sb")
         ln_width = kept([P, KG, PACK], F32, "ln_width")
         probe_sb = kept([P, RG, PACK], BF16, "probe_sb")
@@ -57,7 +54,7 @@ def tile_cosmo_segment_activities_k6_kernel(
         f_scale_raw = kept([P, Q], U8, "f_scale_raw")
         f_scale = kept([P, Q], U8, "f_scale")
         y_scale = [kept([P, RG, J // 2], U8, "y_scale%d" % n) for n in range(2)]
-        e_raw = {(h, g): kept([P, PACK, KP], BF16, "e_raw%d%d" % (h, g)) for h in range(KG) for g in range(KG)}
+        e_raw = {(h, g): passing([P, PACK, KP], BF16, "e_raw", bufs=12, tag="roots") for h in range(KG) for g in range(KG)}
         tau_code = {(h, g): kept([P, KP], I32, "tau_code%d%d" % (h, g)) for h in range(KG) for g in range(KG)}
         tau_scale = {(h, g): kept([P, KP], U8, "tau_scale%d%d" % (h, g)) for h in range(KG) for g in range(KG)}
         h_code = [kept([P, 2 * N], U8, "h_code%d" % g) for g in range(KG)]
@@ -86,7 +83,7 @@ def tile_cosmo_segment_activities_k6_kernel(
             nc.sync.dma_start(out=s_sb[j][:], in_=start[j * P : (j + 1) * P, :])
 
         def tau_exp(h, g):
-            rows = passing([P, PACK, KP], BF16, "tau_rows")
+            rows = passing([P, PACK, KP], BF16, "tau_rows", bufs=4, tag="rows4k")
             for t in range(PACK):
                 nc.scalar.activation(
                     out=rows[:, t, :], in_=e_raw[h, g][:, t, :], func=ACT.Exp, scale=-1.0, bias=ln_width[:, g, t : t + 1]
@@ -94,7 +91,7 @@ def tile_cosmo_segment_activities_k6_kernel(
             live["tau_rows", h, g] = rows
 
         def tau_group(h, g):
-            grouped = passing([P, PACK * KP], BF16, "tau_grouped", bufs=2)
+            grouped = passing([P, PACK * KP], BF16, "tau_grouped", tag="to_quantise")
             nc.vector.tensor_copy(
                 out=grouped[:].rearrange("p (c i t) -> p c t i", i=4, t=PACK),
                 in_=live["tau_rows", h, g][:].rearrange("p t (c i) -> p c t i", i=4),
@@ -107,7 +104,7 @@ def tile_cosmo_segment_activities_k6_kernel(
             )
 
         def w_mul(j):
-            rows = passing([P, N], BF16, "rows")
+            rows = passing([P, N], BF16, "rows", bufs=4)
             nc.vector.tensor_tensor(out=as_pairs(rows[:]), in0=by_pair(p_sb[j][:]), in1=by_pair(s_sb[j][:]), op=MULT)
             live["rows", "w", j] = rows
 
@@ -121,7 +118,7 @@ def tile_cosmo_segment_activities_k6_kernel(
             live["turned", kind, j] = turned
 
         def gather(kind, j, on_scalar):
-            grouped = passing([P, N], BF16, "grouped")
+            grouped = passing([P, N], BF16, "grouped", bufs=4)
             dst = grouped[:].bitcast(F32).rearrange("p (g j u) -> p g j u", g=KG, u=2)
             src = live["turned", kind, j][:].rearrange("p g u j -> p g j u")
             if on_scalar:
@@ -176,7 +173,7 @@ def tile_cosmo_segment_activities_k6_kernel(
             live["v_half", j] = half
 
         def v_mul(j):
-            rows = passing([P, N], BF16, "rows")
+            rows = passing([P, N], BF16, "rows", bufs=4)
             nc.vector.tensor_tensor(out=as_pairs(rows[:]), in0=by_pair(live["v_half", j][:]), in1=by_pair(live["v_other", j][:]), op=MULT)
             live["rows", "v", j] = rows
 
@@ -188,16 +185,16 @@ def tile_cosmo_segment_activities_k6_kernel(
                     in_=live["grouped", "v", j][:, g * KP : (g + 1) * KP],
                 )
 
-        def f_sort(g):
+        def f_sort(G):
+            cols = slice(G * KP, (G + 1) * KP)
+            for g in range(KG):
+                nc.vector.tensor_copy(
+                    out=f_code[g][:, cols].rearrange("p (t c i) -> p c t i", t=PACK, i=4),
+                    in_=f_raw[g][:, cols].rearrange("p (c i t) -> p c t i", t=PACK, i=4),
+                )
             nc.vector.tensor_copy(
-                out=f_code[g][:].rearrange("p (G t c i) -> p G c t i", G=RG, t=PACK, i=4),
-                in_=f_raw[g][:].rearrange("p (G c i t) -> p G c t i", G=RG, t=PACK, i=4),
-            )
-
-        def f_sort_scales():
-            nc.vector.tensor_copy(
-                out=f_scale[:].rearrange("p (G t m) -> p G t m", G=RG, t=PACK),
-                in_=f_scale_raw[:].rearrange("p (G m t) -> p G t m", G=RG, t=PACK),
+                out=f_scale[:, cols].rearrange("p (t m) -> p t m", t=PACK),
+                in_=f_scale_raw[:, cols].rearrange("p (m t) -> p t m", t=PACK),
             )
 
         def r_matmul(n, G, u):
@@ -214,7 +211,7 @@ def tile_cosmo_segment_activities_k6_kernel(
 
         def y_rsqrt(n, G, u):
             if u == 0:
-                live["y_root", n, G] = passing([P, PACK, NJ], F32, "y_root", bufs=6)
+                live["y_root", n, G] = passing([P, PACK, NJ], F32, "y_root", bufs=12, tag="roots")
             for e in range(2):
                 t = 2 * u + e
                 nc.scalar.activation(
@@ -230,7 +227,7 @@ def tile_cosmo_segment_activities_k6_kernel(
 
         def y_store(n, G, i):
             if i == 0:
-                live["y", n, G] = passing([P, GJ, KP], F32, "y", bufs=4)
+                live["y", n, G] = passing([P, GJ, KP], F32, "y", bufs=4, tag="rows4k")
             y = live["y", n, G]
             nc.scalar.activation(
                 out=y[:, i, :].rearrange("j (m t) -> j m t", t=PACK),
@@ -244,7 +241,7 @@ def tile_cosmo_segment_activities_k6_kernel(
                 nc.sync.dma_start(out=rows.rearrange("(i j) r -> j i r", j=P), in_=y[:])
 
         def y_group(n, G):
-            grouped = passing([P, PACK * NJ], BF16, "y_grouped", bufs=3)
+            grouped = passing([P, PACK * NJ], BF16, "y_grouped", tag="to_quantise")
             root = live["y_root", n, G][:].rearrange("p t (c i) -> p c t i", i=2)
             nc.vector.tensor_tensor(
                 out=grouped[:].rearrange("p (c i t) -> p c t i", i=2, t=PACK), in0=root, in1=root, op=MULT
@@ -262,37 +259,40 @@ def tile_cosmo_segment_activities_k6_kernel(
                 rows = out_2[:, 4 * q : 4 * q + 4, n * J // 2 : (n + 1) * J // 2].rearrange("G r m -> r G m")
                 nc.sync.dma_start(out=rows.bitcast(I32), in_=y_scale[n][32 * q : 32 * q + 4, :, :].bitcast(I32))
 
-        nc.vector.memset(one[:], 1.0)
-        nc.vector.memset(h_scale[:].bitcast(I32), 0)
-        nc.vector.memset(f_scale_raw[:].bitcast(I32), 0)
-        nc.scalar.activation(out=warm[:], in_=one[:], func=ACT.Ln)
-        for q in range(4):
-            rows = h_scales[:, 4 * q : 4 * q + 4, :].rearrange("g r n -> r g n")
-            nc.gpsimd.dma_start(out=h_scale[32 * q : 32 * q + 4, :, :].bitcast(I32), in_=rows.bitcast(I32))
-        make_identity(nc, ident[:])
-        nc.sync.dma_start(out=width_sb[:], in_=width.rearrange("(g p t) -> p g t", p=P, t=PACK))
-        load_e(0, 0)
-        load_ps(0)
-        load_e(0, 1)
-        load_ps(1)
-        load_e(1, 0)
-        for g in range(KG):
-            nc.sync.dma_start(out=h_code[g][:].bitcast(I32), in_=h_words[g].bitcast(I32))
-        load_e(1, 1)
-        nc.sync.dma_start(out=probe_sb[:], in_=probe.rearrange("(G p t) -> p G t", p=P, t=PACK))
-        load_ps(2)
-        load_ps(3)
-        for q in range(4):
-            nc.sync.dma_start(
-                out=f_scale_raw[32 * q : 32 * q + 8, :].bitcast(I32), in_=f_scales[:, 4 * q : 4 * q + 4, :].bitcast(I32)
-            )
-        for g in range(KG):
-            nc.sync.dma_start(out=f_raw[g][:], in_=f_words[g].rearrange("p n t -> p (n t)").bitcast(I32))
-        for j in range(4, JT):
-            load_ps(j)
+        with tc.manual_schedule():
+            nc.vector.memset(h_scale[:].bitcast(I32), 0)
+            nc.vector.memset(f_scale_raw[:].bitcast(I32), 0)
+            make_identity(nc, ident[:])
+            nc.sync.dma_start(out=width_sb[:], in_=width.rearrange("(g p t) -> p g t", p=P, t=PACK))
+            load_e(0, 0)
+            load_ps(0)
+            load_e(0, 1)
+            load_ps(1)
+            for q in range(4):
+                rows = h_scales[:, 4 * q : 4 * q + 4, :].rearrange("g r n -> r g n")
+                nc.sync.dma_start(out=h_scale[32 * q : 32 * q + 4, :, :].bitcast(I32), in_=rows.bitcast(I32))
+            load_e(1, 0)
+            for g in range(KG):
+                nc.sync.dma_start(out=h_code[g][:].bitcast(I32), in_=h_words[g].bitcast(I32))
+            load_e(1, 1)
+            load_ps(2)
+            nc.sync.dma_start(out=probe_sb[:], in_=probe.rearrange("(G p t) -> p G t", p=P, t=PACK))
+            load_ps(3)
+            load_ps(4)
+            for q in range(4):
+                nc.sync.dma_start(
+                    out=f_scale_raw[32 * q : 32 * q + 8, :].bitcast(I32), in_=f_scales[:, 4 * q : 4 * q + 4, :].bitcast(I32)
+                )
+            nc.sync.dma_start(out=f_raw[0][:], in_=f_words[0].rearrange("p n t -> p (n t)").bitcast(I32))
+            load_ps(5)
+            nc.sync.dma_start(out=f_raw[1][:], in_=f_words[1].rearrange("p n t -> p (n t)").bitcast(I32))
+            for j in range(6, JT):
+                load_ps(j)
 
+        ctx.enter_context(
+            tc.manual_schedule(engines=set([mybir.EngineType.PE, mybir.EngineType.Activation, mybir.EngineType.DVE]))
+        )
         nc.scalar.activation(out=ln_width[:], in_=width_sb[:], func=ACT.Ln)
-        nc.scalar.activation(out=warm[:], in_=one[:], func=ACT.Exp)
 
         tau_exp(0, 0)
         w_mul(0)
@@ -331,71 +331,135 @@ def tile_cosmo_segment_activities_k6_kernel(
         s_misfit(0, 1, 1)
         s_misfit(1, 1, 1)
         w_mul(3)
+        w_mul(4)
         nc.vector.tensor_tensor(out=probe_inv[:], in0=probe_rsqrt[:], in1=probe_rsqrt[:], op=MULT)
         s_rsqrt(0, 1)
-        s_rsqrt(1, 1)
         v_first(0, True)
+        s_rsqrt(1, 1)
         s_misfit(2, 0, 0)
         s_misfit(2, 0, 1)
         turn("w", 3)
-        f_sort(0)
+        turn("w", 4)
+        s_matmul(2, 1)
+        gather("w", 3, False)
+        gather("w", 4, False)
+        w_quant(3)
+        v_first(1, True)
+        s_rsqrt(2, 0)
+        s_rsqrt(2, 1)
 
         halves = [(n, G, u) for n in range(NG) for G in range(RG) for u in range(2)]
-        R0 = 4
-        CU = 5
+        units = [(n, G) for n in range(NG) for G in range(RG)]
+        MUL = [3,3,4,5,6,7,8,9]
+        FIRST = [2,2,3,4,5,6,7,8]
+        FA = [1,1,1,1,1,0,0,0]
+        RS = [0,0,0,0,0,0,3,6,9,12,15,18,21,24,24,24,24]
+        YS = [0,0,0,0,0,0,0,1,2,3,5,7,9,11,12,12,12]
+        FS = [3,4,5]
 
-        def thirds(first):
-            return halves[max(first, 0) : max(first + 3, 0)]
+        def r_items(k):
+            return halves[RS[k] : RS[k + 1]]
 
-        def mul_tiles(k):
-            return [j for j in range(JT) if k == (j + 2 if j < CU else j + 1)]
+        def t_end(k):
+            return max(RS[k] - 1, 0) if RS[k] < 24 else 24
 
-        for k in range(2, JT + R0 + 3):
-            for j in mul_tiles(k - 1):
-                gather("v", j, k < 8)
-            if k + 1 < JT:
-                gather("w", k + 1, k < 4)
-            if CU <= k - 1 < JT and not (False):
-                v_first(k - 1, False)
-            if k - 2 < CU:
-                v_mul(k - 2)
-            for j in mul_tiles(k - 1):
-                v_quant(j)
-            if k + 1 < JT:
-                w_quant(k + 1)
-            if CU <= k - 1 < JT:
-                v_mul(k - 1)
+        def t_items(k):
+            return halves[t_end(k - 1) : t_end(k)]
+
+        def tiles(L, k):
+            return [j for j in range(len(L)) if L[j] == k]
+
+        def finish(un):
+            y_quant(*un)
+            if un[1] == RG - 1 and un[0] % 2 == 1:
+                y_store_scales(un[0] // 2)
+
+        pending = []
+        ns = 0
+        nt = 0
+        D0 = 10
+        for k in range(3, 15):
+            gv = k<8
+            gw = False
+            if gv:
+                for j in tiles(MUL, k - 1):
+                    gather("v", j, True)
+            if gw and 4 < k + 1 < JT:
+                gather("w", k + 1, True)
+            for j in tiles(FIRST, k):
+                if not FA[j] and MUL[j] == k:
+                    v_first(j, False)
+            for j in tiles(MUL, k):
+                if FIRST[j] < k:
+                    v_mul(j)
             if k + 2 < JT:
                 w_mul(k + 2)
-            if k == 2:
-                f_sort(1)
-            if k == 3:
-                f_sort_scales()
-            if k - 1 < CU:
-                v_first(k - 1, True)
-            done = [(n, G) for (n, G, u) in thirds(3 * (k - R0 - 1)) if u == 1]
-            for item in thirds(3 * (k - R0 - 2) - 1):
-                y_store(*item)
+            for j in tiles(MUL, k):
+                if FIRST[j] == k:
+                    v_mul(j)
+            if not gw and 4 < k + 1 < JT:
+                gather("w", k + 1, False)
+            if not gv:
+                for j in tiles(MUL, k - 1):
+                    gather("v", j, False)
+            for j in tiles(FIRST, k):
+                if not FA[j] and MUL[j] > k:
+                    v_first(j, False)
+            for un in pending:
+                finish(un)
+            pending = []
+            if k + 1 < JT:
+                w_quant(k + 1)
+            for j in tiles(MUL, k - 1):
+                v_quant(j)
+            for G in tiles(FS, k):
+                f_sort(G)
+            for j in tiles(FIRST, k):
+                if FA[j]:
+                    v_first(j, True)
+            done = units[YS[k] : YS[k + 1]]
+            if k < D0:
+                for item in t_items(k - 1):
+                    y_store(*item)
+                    ns = ns + 1
             if k < JT:
-                if k > 2:
-                    s_matmul(k, 0)
+                s_matmul(k, 0)
                 s_matmul(k, 1)
                 s_rsqrt(k, 0)
                 s_rsqrt(k, 1)
-                if k >= CU and (False):
-                    v_first(k, True)
-            for item in thirds(3 * (k - R0)):
-                r_matmul(*item)
-                y_rsqrt(*item)
+            for m in range(RS[k], RS[k + 1]):
+                r_matmul(*halves[m])
+                if k >= D0:
+                    while ns < min(nt, m - 2):
+                        y_store(*halves[ns])
+                        ns = ns + 1
+                y_rsqrt(*halves[m])
+                if k >= D0:
+                    while nt < m - 1:
+                        y_turn(*halves[nt])
+                        nt = nt + 1
+            if k >= D0 and RS[k + 1] == 24:
+                while nt < 24:
+                    y_turn(*halves[nt])
+                    nt = nt + 1
+                    if ns < nt - 1:
+                        y_store(*halves[ns])
+                        ns = ns + 1
+                while ns < 24:
+                    y_store(*halves[ns])
+                    ns = ns + 1
             for un in done:
                 y_group(*un)
+                for un2 in pending:
+                    finish(un2)
+                pending = [un]
             if k + 2 < JT:
                 turn("w", k + 2)
-            for j in mul_tiles(k):
+            for j in tiles(MUL, k):
                 turn("v", j)
-            for item in thirds(3 * (k - R0 - 1) - 1):
-                y_turn(*item)
-            for un in done:
-                y_quant(*un)
-                if un[1] == RG - 1 and un[0] % 2 == 1:
-                    y_store_scales(un[0] // 2)
+            if k < D0:
+                for item in t_items(k):
+                    y_turn(*item)
+                    nt = nt + 1
+        for un in pending:
+            finish(un)

from contextlib import ExitStack

import concourse.mybir as mybir
from concourse.masks import make_identity

J, N, Q = 1024, 1024, 1536
FLOPS = 2 * J * N * (2 * N + Q)

F32 = mybir.dt.float32
BF16 = mybir.dt.bfloat16
I32 = mybir.dt.int32
U8 = mybir.dt.uint8
FP8X4 = mybir.dt.float8_e4m3fn_x4
FP4X4 = mybir.dt.float4_e2m1fn_x4
ACT = mybir.ActivationFunctionType
MULT = mybir.AluOpType.mult

P = 128
PACK = 4
KP = P * PACK
KG = N // KP
RG = Q // KP
JT = J // P
GJ = 2
NG = JT // GJ
NJ = GJ * P


def tile_cosmo_segment_activities_k6_kernel(
    tc, profile, start, energy, width, h_words, h_scales, f_words, f_scales, probe, out_0, out_1, out_2
):
    nc = tc.nc
    with ExitStack() as ctx:
        keep = ctx.enter_context(tc.tile_pool(name="keep", bufs=1))
        work = ctx.enter_context(tc.tile_pool(name="work", bufs=3))
        psum = ctx.enter_context(tc.psum_pool(name="psum", bufs=8))

        def kept(shape, dtype, name):
            return keep.tile(shape, dtype, name=name, align_bytes=64)

        def passing(shape, dtype, name, bufs=3, tag=None):
            return work.tile(shape, dtype, name=name, tag=tag or name, bufs=bufs, align_bytes=64)

        def bank(shape):
            return psum.tile(shape, F32, name="bank")

        ident = kept([P, P], F32, "ident")
        width_sb = kept([P, KG, PACK], BF16, "width_sb")
        ln_width = kept([P, KG, PACK], F32, "ln_width")
        probe_sb = kept([P, RG, PACK], BF16, "probe_sb")
        probe_rsqrt = kept([P, RG, PACK], F32, "probe_rsqrt")
        probe_inv = kept([P, RG, PACK], F32, "probe_inv")
        h_scale = kept([P, KG, N], U8, "h_scale")
        f_scale_raw = kept([P, Q], U8, "f_scale_raw")
        f_scale = kept([P, Q], U8, "f_scale")
        y_scale = [kept([P, RG, J // 2], U8, "y_scale%d" % n) for n in range(2)]
        e_raw = {(h, g): passing([P, PACK, KP], BF16, "e_raw", bufs=12, tag="roots") for h in range(KG) for g in range(KG)}
        tau_code = {(h, g): kept([P, KP], I32, "tau_code%d%d" % (h, g)) for h in range(KG) for g in range(KG)}
        tau_scale = {(h, g): kept([P, KP], U8, "tau_scale%d%d" % (h, g)) for h in range(KG) for g in range(KG)}
        h_code = [kept([P, 2 * N], U8, "h_code%d" % g) for g in range(KG)]
        f_raw = [kept([P, Q], I32, "f_raw%d" % g) for g in range(KG)]
        f_code = [kept([P, Q], I32, "f_code%d" % g) for g in range(KG)]
        p_sb = [kept([P, N], BF16, "p_sb%d" % j) for j in range(JT)]
        s_sb = [kept([P, N], BF16, "s_sb%d" % j) for j in range(JT)]
        w_code = [kept([P, KG, P], I32, "w_code%d" % j) for j in range(JT)]
        w_scale = [kept([P, KG, P], U8, "w_scale%d" % j) for j in range(JT)]
        v_code = {(n, g): kept([P, NJ], I32, "v_code%d%d" % (n, g)) for n in range(NG) for g in range(KG)}
        v_scale = {(n, g): kept([P, NJ], U8, "v_scale%d%d" % (n, g)) for n in range(NG) for g in range(KG)}
        live = {}

        def by_pair(ap):
            return ap.rearrange("j (gm u e) -> j u gm e", u=2, e=2)

        def as_pairs(ap):
            return ap.rearrange("j (u gm e) -> j u gm e", u=2, e=2)

        def load_e(h, g):
            rows = energy[g * KP : (g + 1) * KP, h * KP : (h + 1) * KP]
            nc.sync.dma_start(out=e_raw[h, g][:], in_=rows.rearrange("(p t) l -> p t l", t=PACK))

        def load_ps(j):
            nc.sync.dma_start(out=p_sb[j][:], in_=profile[j * P : (j + 1) * P, :])
            nc.sync.dma_start(out=s_sb[j][:], in_=start[j * P : (j + 1) * P, :])

        def tau_exp(h, g):
            rows = passing([P, PACK, KP], BF16, "tau_rows", bufs=4, tag="rows4k")
            for t in range(PACK):
                nc.scalar.activation(
                    out=rows[:, t, :], in_=e_raw[h, g][:, t, :], func=ACT.Exp, scale=-1.0, bias=ln_width[:, g, t : t + 1]
                )
            live["tau_rows", h, g] = rows

        def tau_group(h, g):
            grouped = passing([P, PACK * KP], BF16, "tau_grouped", tag="to_quantise")
            nc.vector.tensor_copy(
                out=grouped[:].rearrange("p (c i t) -> p c t i", i=4, t=PACK),
                in_=live["tau_rows", h, g][:].rearrange("p t (c i) -> p c t i", i=4),
            )
            live["tau_grouped", h, g] = grouped

        def tau_quant(h, g):
            nc.vector.quantize_mx(
                out=tau_code[h, g][:].bitcast(FP8X4), scales=tau_scale[h, g][:], in_=live["tau_grouped", h, g][:]
            )

        def w_mul(j):
            rows = passing([P, N], BF16, "rows", bufs=4)
            nc.vector.tensor_tensor(out=as_pairs(rows[:]), in0=by_pair(p_sb[j][:]), in1=by_pair(s_sb[j][:]), op=MULT)
            live["rows", "w", j] = rows

        def turn(kind, j):
            words = live["rows", kind, j][:].bitcast(F32)
            turned = bank([P, KG, 2, P])
            for g in range(KG):
                for u in range(2):
                    first = (u * KG + g) * P
                    nc.tensor.transpose(turned[:, g, u, :], words[:, first : first + P], ident[:])
            live["turned", kind, j] = turned

        def gather(kind, j, on_scalar):
            grouped = passing([P, N], BF16, "grouped", bufs=4)
            dst = grouped[:].bitcast(F32).rearrange("p (g j u) -> p g j u", g=KG, u=2)
            src = live["turned", kind, j][:].rearrange("p g u j -> p g j u")
            if on_scalar:
                nc.scalar.copy(out=dst, in_=src)
            else:
                nc.vector.tensor_copy(out=dst, in_=src)
            live["grouped", kind, j] = grouped

        def w_quant(j):
            nc.vector.quantize_mx(
                out=w_code[j][:].rearrange("p g j -> p (g j)").bitcast(FP8X4),
                scales=w_scale[j][:].rearrange("p g j -> p (g j)"),
                in_=live["grouped", "w", j][:],
            )

        def s_excess(j, h):
            acc = bank([P, KP])
            for g in range(KG):
                nc.tensor.matmul_mx(
                    out=acc[:], lhsT=w_code[j][:, g, :].bitcast(FP8X4), lhsT_scale=w_scale[j][:, g, :],
                    rhs=h_code[g][:, 2 * h * KP : 2 * (h + 1) * KP].bitcast(FP4X4),
                    rhs_scale=h_scale[:, g, h * KP : (h + 1) * KP], start=(g == 0), stop=False,
                )
            live["s_acc", j, h] = acc

        def s_misfit(j, h, g):
            nc.tensor.matmul_mx(
                out=live["s_acc", j, h][:], lhsT=w_code[j][:, g, :].bitcast(FP8X4), lhsT_scale=w_scale[j][:, g, :],
                rhs=tau_code[h, g][:].bitcast(FP8X4), rhs_scale=tau_scale[h, g][:], start=False, stop=(g == KG - 1),
            )

        def s_matmul(j, h):
            s_excess(j, h)
            for g in range(KG):
                s_misfit(j, h, g)

        def s_rsqrt(j, h):
            if h == 0:
                live["s_root", j] = passing([P, N], F32, "s_root", bufs=4)
            dst = live["s_root", j][:, h * KP : (h + 1) * KP]
            nc.scalar.activation(out=dst, in_=live["s_acc", j, h][:], func=ACT.Abs_reciprocal_sqrt)

        def v_first(j, on_scalar):
            half = passing([P, N], F32, "v_half")
            root = live["s_root", j]
            if on_scalar:
                nc.scalar.activation(out=half[:], in_=root[:], func=ACT.Square)
                live["v_other", j] = p_sb[j]
            else:
                nc.vector.tensor_tensor(out=half[:], in0=root[:], in1=p_sb[j][:], op=MULT)
                live["v_other", j] = root
            live["v_half", j] = half

        def v_mul(j):
            rows = passing([P, N], BF16, "rows", bufs=4)
            nc.vector.tensor_tensor(out=as_pairs(rows[:]), in0=by_pair(live["v_half", j][:]), in1=by_pair(live["v_other", j][:]), op=MULT)
            live["rows", "v", j] = rows

        def v_quant(j):
            n, first = j // GJ, (j % GJ) * P
            for g in range(KG):
                nc.vector.quantize_mx(
                    out=v_code[n, g][:, first : first + P].bitcast(FP8X4), scales=v_scale[n, g][:, first : first + P],
                    in_=live["grouped", "v", j][:, g * KP : (g + 1) * KP],
                )

        def f_sort(G):
            cols = slice(G * KP, (G + 1) * KP)
            for g in range(KG):
                nc.vector.tensor_copy(
                    out=f_code[g][:, cols].rearrange("p (t c i) -> p c t i", t=PACK, i=4),
                    in_=f_raw[g][:, cols].rearrange("p (c i t) -> p c t i", t=PACK, i=4),
                )
            nc.vector.tensor_copy(
                out=f_scale[:, cols].rearrange("p (t m) -> p t m", t=PACK),
                in_=f_scale_raw[:, cols].rearrange("p (m t) -> p t m", t=PACK),
            )

        def r_matmul(n, G, u):
            acc = bank([P, 2, NJ])
            for e in range(2):
                first = G * KP + (2 * u + e) * P
                for g in range(KG):
                    nc.tensor.matmul_mx(
                        out=acc[:, e, :], lhsT=f_code[g][:, first : first + P].bitcast(FP8X4),
                        lhsT_scale=f_scale[PACK * g :, first : first + P],
                        rhs=v_code[n, g][:].bitcast(FP8X4), rhs_scale=v_scale[n, g][:], start=(g == 0), stop=(g == KG - 1),
                    )
            live["r_acc", n, G, u] = acc

        def y_rsqrt(n, G, u):
            if u == 0:
                live["y_root", n, G] = passing([P, PACK, NJ], F32, "y_root", bufs=12, tag="roots")
            for e in range(2):
                t = 2 * u + e
                nc.scalar.activation(
                    out=live["y_root", n, G][:, t, :], in_=live["r_acc", n, G, u][:, e, :], func=ACT.Abs_reciprocal_sqrt,
                    scale=probe_inv[:, G, t : t + 1],
                )

        def y_turn(n, G, i):
            turned = bank([P, PACK, P])
            for t in range(PACK):
                nc.tensor.transpose(turned[:, t, :], live["y_root", n, G][:, t, i * P : (i + 1) * P], ident[:])
            live["y_turned", n, G, i] = turned

        def y_store(n, G, i):
            if i == 0:
                live["y", n, G] = passing([P, GJ, KP], F32, "y", bufs=4, tag="rows4k")
            y = live["y", n, G]
            nc.scalar.activation(
                out=y[:, i, :].rearrange("j (m t) -> j m t", t=PACK),
                in_=live["y_turned", n, G, i][:].rearrange("j t m -> j m t"), func=ACT.Square,
            )
            if (n, G) == (NG - 1, RG - 1):
                j = n * GJ + i
                nc.sync.dma_start(out=out_0[j * P : (j + 1) * P, G * KP : (G + 1) * KP], in_=y[:, i, :])
            elif i == GJ - 1:
                rows = out_0[n * NJ : (n + 1) * NJ, G * KP : (G + 1) * KP]
                nc.sync.dma_start(out=rows.rearrange("(i j) r -> j i r", j=P), in_=y[:])

        def y_group(n, G):
            grouped = passing([P, PACK * NJ], BF16, "y_grouped", tag="to_quantise")
            root = live["y_root", n, G][:].rearrange("p t (c i) -> p c t i", i=2)
            nc.vector.tensor_tensor(
                out=grouped[:].rearrange("p (c i t) -> p c t i", i=2, t=PACK), in0=root, in1=root, op=MULT
            )
            live["y_grouped", n, G] = grouped

        def y_quant(n, G):
            code = passing([P, NJ], I32, "y_code", bufs=4)
            nc.vector.quantize_mx(out=code[:].bitcast(FP8X4), scales=y_scale[n // 2][:, G, (n % 2) * NJ : (n % 2 + 1) * NJ], in_=live["y_grouped", n, G][:])
            words = out_1[G].rearrange("p m t -> p (m t)").bitcast(I32)
            nc.sync.dma_start(out=words[:, n * NJ : (n + 1) * NJ], in_=code[:])

        def y_store_scales(n):
            for q in range(4):
                rows = out_2[:, 4 * q : 4 * q + 4, n * J // 2 : (n + 1) * J // 2].rearrange("G r m -> r G m")
                nc.sync.dma_start(out=rows.bitcast(I32), in_=y_scale[n][32 * q : 32 * q + 4, :, :].bitcast(I32))

        with tc.manual_schedule():
            nc.vector.memset(h_scale[:].bitcast(I32), 0)
            nc.vector.memset(f_scale_raw[:].bitcast(I32), 0)
            make_identity(nc, ident[:])
            nc.sync.dma_start(out=width_sb[:], in_=width.rearrange("(g p t) -> p g t", p=P, t=PACK))
            load_e(0, 0)
            load_ps(0)
            load_e(0, 1)
            load_ps(1)
            for q in range(4):
                rows = h_scales[:, 4 * q : 4 * q + 4, :].rearrange("g r n -> r g n")
                nc.sync.dma_start(out=h_scale[32 * q : 32 * q + 4, :, :].bitcast(I32), in_=rows.bitcast(I32))
            load_e(1, 0)
            for g in range(KG):
                nc.sync.dma_start(out=h_code[g][:].bitcast(I32), in_=h_words[g].bitcast(I32))
            load_e(1, 1)
            load_ps(2)
            nc.sync.dma_start(out=probe_sb[:], in_=probe.rearrange("(G p t) -> p G t", p=P, t=PACK))
            load_ps(3)
            load_ps(4)
            for q in range(4):
                nc.sync.dma_start(
                    out=f_scale_raw[32 * q : 32 * q + 8, :].bitcast(I32), in_=f_scales[:, 4 * q : 4 * q + 4, :].bitcast(I32)
                )
            nc.sync.dma_start(out=f_raw[0][:], in_=f_words[0].rearrange("p n t -> p (n t)").bitcast(I32))
            load_ps(5)
            nc.sync.dma_start(out=f_raw[1][:], in_=f_words[1].rearrange("p n t -> p (n t)").bitcast(I32))
            for j in range(6, JT):
                load_ps(j)

        ctx.enter_context(
            tc.manual_schedule(engines=set([mybir.EngineType.PE, mybir.EngineType.Activation, mybir.EngineType.DVE]))
        )
        nc.scalar.activation(out=ln_width[:], in_=width_sb[:], func=ACT.Ln)

        tau_exp(0, 0)
        w_mul(0)
        turn("w", 0)
        gather("w", 0, False)
        tau_group(0, 0)
        w_quant(0)
        w_mul(1)
        turn("w", 1)
        tau_quant(0, 0)
        tau_exp(0, 1)
        tau_group(0, 1)
        gather("w", 1, False)
        tau_quant(0, 1)
        s_matmul(0, 0)
        w_quant(1)
        s_matmul(1, 0)
        s_excess(0, 1)
        s_excess(1, 1)
        tau_exp(1, 0)
        tau_group(1, 0)
        w_mul(2)
        turn("w", 2)
        tau_quant(1, 0)
        s_misfit(0, 1, 0)
        s_misfit(1, 1, 0)
        tau_exp(1, 1)
        nc.scalar.activation(out=probe_rsqrt[:], in_=probe_sb[:], func=ACT.Abs_reciprocal_sqrt)
        tau_group(1, 1)
        gather("w", 2, True)
        s_rsqrt(0, 0)
        s_rsqrt(1, 0)
        w_quant(2)
        tau_quant(1, 1)
        s_excess(2, 0)
        s_misfit(0, 1, 1)
        s_misfit(1, 1, 1)
        w_mul(3)
        w_mul(4)
        nc.vector.tensor_tensor(out=probe_inv[:], in0=probe_rsqrt[:], in1=probe_rsqrt[:], op=MULT)
        s_rsqrt(0, 1)
        v_first(0, True)
        s_rsqrt(1, 1)
        s_misfit(2, 0, 0)
        s_misfit(2, 0, 1)
        turn("w", 3)
        turn("w", 4)
        s_matmul(2, 1)
        gather("w", 3, False)
        gather("w", 4, False)
        w_quant(3)
        v_first(1, True)
        s_rsqrt(2, 0)
        s_rsqrt(2, 1)

        halves = [(n, G, u) for n in range(NG) for G in range(RG) for u in range(2)]
        units = [(n, G) for n in range(NG) for G in range(RG)]
        MUL = [3,3,4,5,6,7,8,9]
        FIRST = [2,2,3,4,5,6,7,8]
        FA = [1,1,1,1,1,0,0,0]
        RS = [0,0,0,0,0,0,3,6,9,12,15,18,21,24,24,24,24]
        YS = [0,0,0,0,0,0,0,1,2,3,5,7,9,11,12,12,12]
        FS = [3,4,5]

        def r_items(k):
            return halves[RS[k] : RS[k + 1]]

        def t_end(k):
            return max(RS[k] - 1, 0) if RS[k] < 24 else 24

        def t_items(k):
            return halves[t_end(k - 1) : t_end(k)]

        def tiles(L, k):
            return [j for j in range(len(L)) if L[j] == k]

        def finish(un):
            y_quant(*un)
            if un[1] == RG - 1 and un[0] % 2 == 1:
                y_store_scales(un[0] // 2)

        pending = []
        ns = 0
        nt = 0
        D0 = 10
        for k in range(3, 15):
            gv = k<8
            gw = False
            if gv:
                for j in tiles(MUL, k - 1):
                    gather("v", j, True)
            if gw and 4 < k + 1 < JT:
                gather("w", k + 1, True)
            for j in tiles(FIRST, k):
                if not FA[j] and MUL[j] == k:
                    v_first(j, False)
            for j in tiles(MUL, k):
                if FIRST[j] < k:
                    v_mul(j)
            if k + 2 < JT:
                w_mul(k + 2)
            for j in tiles(MUL, k):
                if FIRST[j] == k:
                    v_mul(j)
            if not gw and 4 < k + 1 < JT:
                gather("w", k + 1, False)
            if not gv:
                for j in tiles(MUL, k - 1):
                    gather("v", j, False)
            for j in tiles(FIRST, k):
                if not FA[j] and MUL[j] > k:
                    v_first(j, False)
            for un in pending:
                finish(un)
            pending = []
            if k + 1 < JT:
                w_quant(k + 1)
            for j in tiles(MUL, k - 1):
                v_quant(j)
            for G in tiles(FS, k):
                f_sort(G)
            for j in tiles(FIRST, k):
                if FA[j]:
                    v_first(j, True)
            done = units[YS[k] : YS[k + 1]]
            if k < D0:
                for item in t_items(k - 1):
                    y_store(*item)
                    ns = ns + 1
            if k < JT:
                s_matmul(k, 0)
                s_matmul(k, 1)
                s_rsqrt(k, 0)
                s_rsqrt(k, 1)
            for m in range(RS[k], RS[k + 1]):
                r_matmul(*halves[m])
                if k >= D0:
                    while ns < min(nt, m - 2):
                        y_store(*halves[ns])
                        ns = ns + 1
                y_rsqrt(*halves[m])
                if k >= D0:
                    while nt < m - 1:
                        y_turn(*halves[nt])
                        nt = nt + 1
            if k >= D0 and RS[k + 1] == 24:
                while nt < 24:
                    y_turn(*halves[nt])
                    nt = nt + 1
                    if ns < nt - 1:
                        y_store(*halves[ns])
                        ns = ns + 1
                while ns < 24:
                    y_store(*halves[ns])
                    ns = ns + 1
            for un in done:
                y_group(*un)
                for un2 in pending:
                    finish(un2)
                pending = [un]
            if k + 2 < JT:
                turn("w", k + 2)
            for j in tiles(MUL, k):
                turn("v", j)
            if k < D0:
                for item in t_items(k):
                    y_turn(*item)
                    nt = nt + 1
        for un in pending:
            finish(un)
